import numpy as np, ml_dtypes
CORES = [16,32,48,64,80]
N = 5
TK = 32
def setup_inputs(rng):
    rt = (0.75 * rng.standard_normal((128, 1), dtype=np.float32) + rng.standard_normal((128, N), dtype=np.float32) / 2).astype(ml_dtypes.bfloat16)
    return {"x": rng.standard_normal((N, 128, TK), dtype=np.float32).astype(ml_dtypes.bfloat16), "rt": np.broadcast_to(rt, (N, 128, N)).copy(), "w": rng.standard_normal((N, 128, 128), dtype=np.float32).astype(ml_dtypes.bfloat16)}
def setup_inputs_big(rng):
    d = setup_inputs(rng)
    for k in ("x", "w"): d[k] = (d[k].astype(np.float32) * 1024.0).astype(d[k].dtype)
    return d
def setup_inputs_small(rng):
    d = setup_inputs(rng)
    for k in ("x", "w"): d[k] = (d[k].astype(np.float32) * (1 / 1024.0)).astype(d[k].dtype)
    return d
def reference(x, rt, w):
    X, RT, W = x.astype(np.float64), rt.astype(np.float64), w.astype(np.float64)
    y = np.zeros((N, 128, TK))
    for r in range(N):
        sc = RT[r].T @ X[r]
        g = np.exp(sc - sc.max(axis=0)); g = g / g.sum(axis=0)
        y[r] = sum(g[j] * (W[j].T @ X[r]) for j in range(N))
    return {"y": y.astype(ml_dtypes.bfloat16)}

from concourse.bass import DstId, RemoteDMATransfer
from concourse.mybir import AluOpType, AxisListType, ActivationFunctionType

N = 5
TK = 32
D = 128

SCRATCH = {
    "wall": ("sbuf", [128, N * D], "bfloat16"),
    "xs": ("sbuf", [128, TK], "bfloat16"),
    "rts": ("sbuf", [128, N], "bfloat16"),
    "ident": ("sbuf", [128, 128], "bfloat16"),
    "negm": ("sbuf", [128, 1], "float32"),
    "ex": ("sbuf", [128, N], "float32"),
    "ssum": ("sbuf", [128, 1], "float32"),
    "rs": ("sbuf", [128, 1], "float32"),
    "dg": ("sbuf", [128, N * TK], "bfloat16"),
    "xts": ("sbuf", [128, D], "bfloat16"),
    "xg": ("sbuf", [128, N * TK], "bfloat16"),
    "ys": ("sbuf", [128, TK], "bfloat16"),
    "scp": ("psum", [128, 512], "float32"),
    "xtp": ("psum", [128, 512], "float32"),
    "xgp": ("psum", [128, 512], "float32"),
    "acc": ("psum", [128, 512], "float32"),
}
SEMAPHORES = ["s_w", "s_x", "s_ms", "s_id", "s_sc", "s_negm", "s_exp", "s_rs", "s_xtp", "s_xts", "s_dg", "s_xgp",
              "s_xg", "s_acc", "s_y", "s_st", "s_sent"] + ["arr%d" % k for k in range(N)]


def _bits(m):
    return sum(1 for b in range(16) if (m >> b) & 1)


def rank_program(g, core, T, topo):
    r = T.rank_of(core)
    if r is None:
        return
    S = T.sem
    cores = T.cores

    def slot(j):
        return T.wall[:, j * D:(j + 1) * D]

    def blk(t, j):
        return t[:, j * TK:(j + 1) * TK]

    g.sync.dma_start(slot(r), T.w[:, :]).then_inc(S.s_w, 16)
    g.scalar.dma_start(T.xs[:, :], T.x[:, :]).then_inc(S.s_x, 16)
    g.scalar.dma_start(T.rts[:, :], T.rt[:, :]).then_inc(S.s_x, 16)

    g.vector.memset(T.ident[:, :], 1.0).then_inc(S.s_ms, 1)
    g.wait_ge(S.s_ms, 1)
    g.affine_select(T.ident[:, :], T.ident[:, :], [[-1, 128]], AluOpType.is_equal, 0.0, 0, 1).then_inc(S.s_id, 1)

    order = [(r + k) % N for k in range(1, N)]
    mask = 0xFFFF
    for j in order:
        assert topo.may_write(core, cores[j])
        mask &= topo.mask(core, cores[j])
    eng = _bits(mask)
    ids = []
    for j in order:
        rid, pid, _se = topo.addr(cores[j])
        ids.append(DstId(rid=rid, pnc=pid))
    g.wait_ge(S.s_w, 16)
    g.remote_dma_fused([RemoteDMATransfer(dst_ids=ids, dma_engine_mask=mask, remote_sem=S["arr%d" % r],
                                          srcs=[slot(r)], dsts=[slot(r) for _ in order], alu_op=0)],
                       local_sem=S.s_sent)

    te, ve, se = g.tensor, g.vector, g.scalar
    te.wait_ge(S.s_x, 32)
    te.matmul(T.scp[0:TK, 0:N], T.xs[:, :], T.rts[:, :], True, True).then_inc(S.s_sc, 1)
    te.wait_ge(S.s_id, 1)
    te.matmul(T.xtp[0:TK, 0:D], T.xs[:, :], T.ident[:, :], True, True).then_inc(S.s_xtp, 1)

    ve.wait_ge(S.s_sc, 1)
    ve.tensor_reduce(T.negm[0:TK, :], T.scp[0:TK, 0:N], AxisListType.X, AluOpType.max,
                     negate=True).then_inc(S.s_negm, 1)
    se.wait_ge(S.s_negm, 1)
    se.activation(T.ex[0:TK, :], T.scp[0:TK, 0:N], ActivationFunctionType.Exp, bias=T.negm[0:TK, :], scale=1.0,
                  accum_out=T.ssum[0:TK, :]).then_inc(S.s_exp, 1)
    ve.wait_ge(S.s_xtp, 1)
    ve.tensor_copy(T.xts[0:TK, :], T.xtp[0:TK, 0:D]).then_inc(S.s_xts, 1)
    ve.wait_ge(S.s_exp, 1)
    ve.reciprocal(T.rs[0:TK, :], T.ssum[0:TK, :]).then_inc(S.s_rs, 1)
    ve.wait_ge(S.s_rs, 1)
    ve.wait_ge(S.s_id, 1)
    for j in range(N):
        ve.tensor_scalar(T.dg[0:TK, j * TK:(j + 1) * TK], T.ident[0:TK, 0:TK], T.ex[0:TK, j:j + 1],
                         T.rs[0:TK, :], AluOpType.mult, AluOpType.mult).then_inc(S.s_dg, 1)
    te.wait_ge(S.s_xts, 1)
    te.wait_ge(S.s_dg, N)
    te.matmul(T.xgp[:, 0:N * TK], T.xts[0:TK, :], T.dg[0:TK, :], True, True).then_inc(S.s_xgp, 1)
    ve.wait_ge(S.s_xgp, 1)
    ve.tensor_copy(T.xg[:, :], T.xgp[:, 0:N * TK]).then_inc(S.s_xg, 1)

    te.wait_ge(S.s_xg, 1)
    te.wait_ge(S.s_w, 16)
    te.matmul(T.acc[:, 0:TK], slot(r), blk(T.xg, r), True, False)
    for k in range(1, N):
        j = (r - k) % N
        te.wait_ge(S["arr%d" % j], eng)
        mm = te.matmul(T.acc[:, 0:TK], slot(j), blk(T.xg, j), False, k == N - 1)
    mm.then_inc(S.s_acc, 1)

    ve.wait_ge(S.s_acc, 1)
    ve.tensor_copy(T.ys[:, :], T.acc[:, 0:TK]).then_inc(S.s_y, 1)
    g.sync.wait_ge(S.s_y, 1)
    g.sync.dma_start(T.y[:, :], T.ys[:, :]).then_inc(S.s_st, 16)
    g.sync.wait_ge(S.s_st, 16)
    g.wait_ge(S.s_sent, eng)
